import numpy as np
import ml_dtypes


def mxq(x, axis, fmt="e4m3"):
    dtype, down = {"e4m3": (ml_dtypes.float8_e4m3fn, 7), "e5m2": (ml_dtypes.float8_e5m2, 14)}[fmt]
    v = np.moveaxis(np.asarray(x, np.float32).astype(ml_dtypes.bfloat16).astype(np.float64), axis, -1)
    blocks = v.reshape(v.shape[:-1] + (-1, 32))
    amax = np.abs(blocks).max(-1, keepdims=True)
    byte = np.maximum(np.where(amax > 0, np.frexp(amax)[1] - 1 + 127, 0) - down, 1)
    scale = np.exp2(byte - 127.0)
    codes = (blocks / scale).astype(np.float32).astype(dtype).astype(np.float64)
    return np.moveaxis((codes * scale).reshape(v.shape), -1, axis)


WIDE = False


def mx_kscale(k):
    if not WIDE:
        return np.ones(k)
    levels = np.array([10, -10, 5, -5, 0])
    if k % 512:
        return np.exp2(np.random.permutation(np.resize(levels, k // 32))).repeat(32)
    a = np.empty((k // 512, 16))
    for p in range(k // 512):
        a[p, :8] = np.random.permutation(np.resize(levels, 8))
        for g in range(8):
            far = levels[np.abs(levels - a[p, g]) >= 10]
            a[p, g + 8] = far[np.random.randint(len(far))]
    return np.exp2(a.ravel()).repeat(32)


def f64(x):
    return np.asarray(x).astype(np.float64)


def striped(idx):
    return np.tile(idx.reshape(-1, 16).T, (8, 1)).astype(np.uint16)


def unstriped(offs):
    return offs[:16].T.reshape(-1).astype(np.int64)


def pack_weight(w):
    k, n = w.shape
    w = f64(np.asarray(w, np.float32).astype(ml_dtypes.bfloat16)).reshape(k // 32, 32, n)
    amax = np.abs(w).max(1)
    byte = np.clip(np.where(amax > 0, np.frexp(amax)[1] - 1 + 127 - 7, 1), 1, 254)
    scaled = (w * np.exp2(127.0 - byte)[:, None, :]).reshape(k, n).astype(np.float32)
    words = np.ascontiguousarray(scaled.reshape(k // 512, 128, 4, n).transpose(0, 1, 3, 2)).astype(ml_dtypes.float8_e4m3fn).view(np.uint8)
    return words, np.ascontiguousarray(byte.astype(np.uint8).reshape(k // 512, 16, n))


def unpack_weight(words, scales):
    g, p, n, _ = words.shape
    vals = np.ascontiguousarray(words).view(ml_dtypes.float8_e4m3fn).astype(np.float64) * np.repeat(np.exp2(scales.astype(np.float64) - 127.0), 8, axis=1)[..., None]
    return vals.transpose(0, 1, 3, 2).reshape(g * 512, n)


K, T, S, N, D = 1024, 2048, 512, 256, 3
P = 2 ** 7


def setup_inputs():
    n = np.random.standard_normal
    s = mx_kscale(K)[:, None]
    packed_xT = pack_weight(n((K, T)) * s)
    return {
        "x_words": packed_xT[0],
        "x_scales": packed_xT[1],
        "w1": (n((K, N)) / np.sqrt(K) / s).astype(np.float32),
        "w2": (n((K, N)) / np.sqrt(K) / s).astype(np.float32),
        "cpl": (np.tile(np.random.uniform(0.1, 0.7, (D, 1, S)), (1, P, 1))).astype(np.float32),
        "freq": (n((N, S)) * 0.5).astype(np.float32),
        "offs": striped(np.random.permutation(T)[:S]),
        "pos1": striped(np.random.permutation(S)[:S]),
        "pos2": striped(np.random.permutation(S)[:S]),
        "pos3": striped(np.random.permutation(S)[:S]),
    }


def reference(x_words, x_scales, w1, w2, cpl, freq, offs, pos1, pos2, pos3):
    xq = unpack_weight(x_words, x_scales)[:, unstriped(offs)]
    y = mxq(f64(w1), 0, "e4m3").T @ xq
    z = mxq(f64(w2), 0, "e4m3").T @ xq
    rr = np.sqrt((y) ** 2 + (z) ** 2 + 0.1)
    cs = y / rr
    sn = z / rr
    msn = sn[:, unstriped(pos1)] * f64(cpl)[0, :1] + sn[:, unstriped(pos2)] * f64(cpl)[1, :1] + sn[:, unstriped(pos3)] * f64(cpl)[2, :1]
    mc = cs[:, unstriped(pos1)] * f64(cpl)[0, :1] + cs[:, unstriped(pos2)] * f64(cpl)[1, :1] + cs[:, unstriped(pos3)] * f64(cpl)[2, :1]
    tq = cs * msn - (sn * mc)
    dth = f64(freq) + tq
    return (cs - (0.4 * (dth * sn))) / (np.sqrt(0.16 * ((dth) ** 2) + 1.0))

@@ -1,0 +1,281 @@
+from contextlib import ExitStack
+
+import concourse.mybir as mybir
+from concourse.masks import make_identity
+
+K, T, S, N, D = 1024, 2048, 512, 256, 3
+P = 128
+PACK = 4
+K_PASS = P * PACK
+PASSES = K // K_PASS
+BLOCKS = N // P
+TILES = S // P
+SPARE = 8
+FLOPS = 2 * 2 * K * N * S
+
+F32 = mybir.dt.float32
+BF16 = mybir.dt.bfloat16
+I32 = mybir.dt.int32
+U32 = mybir.dt.uint32
+U16 = mybir.dt.uint16
+U8 = mybir.dt.uint8
+FP8X4 = mybir.dt.float8_e4m3fn_x4
+ACT = mybir.ActivationFunctionType
+MULT = mybir.AluOpType.mult
+ADD = mybir.AluOpType.add
+
+
+def tile_picked_yphas_step_p_kernel(
+    tc, x_words, x_scales, w1, w2, cpl, freq, offs, pos1, pos2, pos3, out
+):
+    nc = tc.nc
+    with ExitStack() as ctx:
+        keep = ctx.enter_context(tc.tile_pool(name="keep", bufs=1))
+        psum = ctx.enter_context(tc.psum_pool(name="psum", bufs=1))
+
+        def held(name, shape, dtype):
+            return keep.tile(shape, dtype, name=name, align_bytes=64)
+
+        x_tab = [held("x_tab%d" % o, [P, T], I32) for o in range(PASSES)]
+        s_tab = held("s_tab", [P, T], U8)
+        offs_sb = held("offs_sb", [P, S // 16], U16)
+        pos_sb = [held("pos_sb%d" % d, [P, S // 16], U16) for d in range(D)]
+        w_raw = {
+            (b, i, o): held("w_raw%d%d%d" % (b, i, o), [P, PACK, P], F32)
+            for b in range(BLOCKS) for i in range(2) for o in range(PASSES)
+        }
+        freq_sb = [held("freq_sb%d" % b, [P, S], F32) for b in range(BLOCKS)]
+        cpl_rows = held("cpl_rows", [P, D, P], F32)
+        ident = held("ident", [P, P], F32)
+        warm = held("warm", [P, 8], F32)
+
+        nc.vector.memset(s_tab[:].bitcast(I32), 0)
+        nc.vector.memset(warm[:], 1.0)
+        nc.scalar.activation(warm[:, 0:1], warm[:, 1:2], ACT.Abs_reciprocal_sqrt)
+        make_identity(nc, ident[:])
+        nc.gpsimd.memset(cpl_rows[:], 0.0)
+
+        def load_x(o):
+            nc.sync.dma_start(x_tab[o][:], x_words[o].rearrange("p c r -> p (c r)").bitcast(I32))
+
+        def load_w(b, i, o):
+            rows = (w1, w2)[i][o * K_PASS : (o + 1) * K_PASS, b * P : (b + 1) * P]
+            nc.sync.dma_start(w_raw[b, i, o][:], rows.rearrange("(p j) n -> p j n", j=PACK))
+
+        load_x(0)
+        nc.sync.dma_start(offs_sb[:], offs)
+        for q in range(4):
+            nc.sync.dma_start(
+                s_tab[32 * q : 32 * q + 4 * PASSES, :].bitcast(I32),
+                x_scales[:, 4 * q : 4 * q + 4, :].bitcast(I32),
+            )
+        load_x(1)
+        for o in range(PASSES):
+            for i in range(2):
+                load_w(0, i, o)
+        nc.sync.dma_start(cpl_rows[0:TILES, :, :], cpl[:, 0, :].rearrange("d (t p) -> t d p", p=P))
+        for o in range(PASSES):
+            for i in range(2):
+                load_w(1, i, o)
+        for d, pos in enumerate((pos1, pos2, pos3)):
+            nc.sync.dma_start(pos_sb[d][:], pos)
+        for b in range(BLOCKS):
+            nc.sync.dma_start(freq_sb[b][:], freq[b * P : (b + 1) * P, :])
+
+        def shared(tag, name, shape, dtype):
+            return keep.tile(shape, dtype, name=name, tag=tag, align_bytes=64)
+
+        def bank(tag, name):
+            return psum.tile([P, S], F32, name=name, tag=tag)
+
+        x_codes = [held("x_codes%d" % o, [P, S], U32) for o in range(PASSES)]
+        x_bytes = held("x_bytes", [P, S], U8)
+        nc.vector.tensor_copy(x_codes[0][:], x_tab[0][:].bitcast(U32).indirect(offs_sb[:]))
+        nc.vector.tensor_copy(x_bytes[:], s_tab[:].indirect(offs_sb[:]))
+        nc.vector.tensor_copy(x_codes[1][:], x_tab[1][:].bitcast(U32).indirect(offs_sb[:]))
+
+        w_codes, w_bytes = {}, {}
+
+        def interleave(grouped, b, i, o, copy):
+            copy(
+                grouped.rearrange("p (c n) j -> p c j n", n=4),
+                w_raw[b, i, o][:].rearrange("p j (c n) -> p c j n", n=4),
+            )
+
+        def quantise(name, grouped, keys):
+            codes = held("w_codes" + name, [P, len(keys) * P], U32)
+            planes = held("w_bytes" + name, [P, len(keys) * P], U8)
+            nc.vector.quantize_mx(
+                out=codes[:].bitcast(FP8X4), scales=planes[:], in_=grouped.rearrange("p n j -> p (n j)")
+            )
+            for n, key in enumerate(keys):
+                w_codes[key] = codes[:, n * P : (n + 1) * P]
+                w_bytes[key] = planes[:, n * P : (n + 1) * P]
+
+        cs = [held("cs%d" % b, [P, S + SPARE], F32) for b in range(BLOCKS)]
+        sn = [held("sn%d" % b, [P, S + SPARE], F32) for b in range(BLOCKS)]
+        nsn = [held("nsn%d" % b, [P, S], F32) for b in range(BLOCKS)]
+        for b in range(BLOCKS):
+            nc.gpsimd.memset(cs[b][:, S:], 0.0)
+            nc.gpsimd.memset(sn[b][:, S:], 0.0)
+
+        def products(b, z_tags):
+            width = S // len(z_tags)
+            cuts = [slice(h * width, (h + 1) * width) for h in range(len(z_tags))]
+            y = bank("B0", "y%d" % b)
+            z = [bank(tag, "z%d%s" % (b, tag)) for tag in z_tags]
+            groups = [(0, y, slice(0, S))] + [(1, zh, c) for zh, c in zip(z, cuts)]
+            for o in range(PASSES):
+                for i, acc, c in groups:
+                    nc.tensor.matmul_mx(
+                        out=acc[:, c],
+                        lhsT=w_codes[b, i, o].bitcast(FP8X4),
+                        lhsT_scale=w_bytes[b, i, o],
+                        rhs=x_codes[o][:, c].bitcast(FP8X4),
+                        rhs_scale=x_bytes[4 * o :, c],
+                        start=(o == 0),
+                        stop=(o == PASSES - 1),
+                    )
+            return y, z, cuts
+
+        def radius(b, y, z, cuts):
+            sq = [shared("sq%d%d" % (b, i), "sq%d%d" % (b, i), [P, S], F32) for i in range(2)]
+            r2 = shared("r2%d" % b, "r2%d" % b, [P, S], F32)
+            rinv = shared("rinv%d" % b, "rinv%d" % b, [P, S], F32)
+            nc.scalar.activation(sq[0][:], y[:], ACT.Square)
+            for zh, c in zip(z, cuts):
+                nc.scalar.activation(sq[1][:, c], zh[:, c], ACT.Square)
+            for c in cuts:
+                nc.vector.tensor_tensor(r2[:, c], sq[0][:, c], sq[1][:, c], ADD)
+            for c in cuts:
+                nc.scalar.activation(rinv[:, c], r2[:, c], ACT.Abs_reciprocal_sqrt, bias=0.1)
+            return rinv
+
+        def normalise(b, y, z, cuts, rinv):
+            for zh, c in zip(z, cuts):
+                nc.vector.tensor_tensor(sn[b][:, c], zh[:, c], rinv[:, c], MULT)
+                nc.vector.tensor_tensor(cs[b][:, c], y[:, c], rinv[:, c], MULT)
+            nc.scalar.activation(nsn[b][:], sn[b][:, :S], ACT.Copy, scale=-1.0)
+
+        cpl_t = held("cpl_t", [P, D, TILES], F32)
+
+        def turn_cpl():
+            turned = bank("B5", "cpl_turned")
+            for d in range(D):
+                nc.tensor.transpose(turned[:, d * P : (d + 1) * P], cpl_rows[:, d, :], ident[:])
+            nc.scalar.copy(cpl_t[:], turned[:].rearrange("p (d r) -> p d r", r=P)[:, 0:D, 0:TILES])
+
+        def turn_freq(b, tag):
+            turned = bank("B5", "freq_turned%d" % b)
+            for t in range(TILES):
+                nc.tensor.transpose(turned[:, t * P : (t + 1) * P], freq_sb[b][:, t * P : (t + 1) * P], ident[:])
+            freq_t = shared(tag, "freq_t%d" % b, [P, S], F32)
+            nc.scalar.copy(freq_t[:], turned[:])
+            return freq_t
+
+        def tile_cols(t0, t1):
+            return slice(t0 * P, t1 * P)
+
+        def add_turned(dst, srcs, t0, t1, opens=False, closes=False):
+            steps = [(src, tile_cols(t, t + 1)) for src in srcs for t in range(t0, t1)]
+            for n, (src, c) in enumerate(steps):
+                nc.tensor.matmul(
+                    dst[:, c], lhsT=src[:, c], rhs=ident[:], is_transpose=True,
+                    start=(opens and n == 0), stop=(closes and n == len(steps) - 1),
+                )
+
+        def gather_sn(b, d, v):
+            nc.vector.tensor_tensor(v, sn[b][:].indirect(pos_sb[d][:]), cs[b][:, :S], MULT)
+
+        def gather_cs(b, d, x, t0, t1):
+            places = pos_sb[d][:, t0 * P // 16 : t1 * P // 16]
+            nc.vector.tensor_tensor(x[:, tile_cols(t0, t1)], cs[b][:].indirect(places), nsn[b][:, tile_cols(t0, t1)], MULT)
+
+        def weigh(d, f, cross, t0, t1):
+            for t in range(t0, t1):
+                c = tile_cols(t, t + 1)
+                nc.scalar.activation(f[:, c], cross[:, c], ACT.Copy, scale=cpl_t[:, d, t : t + 1])
+
+        def neighbour(b, d, v, x):
+            cross = bank("B%d" % (2 + d), "cross%d%d" % (b, d))
+            gather_sn(b, d, v)
+            add_turned(cross, [v], 0, TILES, opens=True)
+            gather_cs(b, d, x, 0, TILES)
+            add_turned(cross, [x], 0, TILES, closes=True)
+            weigh(d, f[b][d], cross, 0, TILES)
+
+        def damping(b, dth, t0, t1):
+            c = tile_cols(t0, t1)
+            a2, q = [held("%s%d%d" % (n, b, t0), [P, S], F32) for n in ("a2", "q")]
+            nc.scalar.activation(a2[:, c], dth[:, c], ACT.Square, scale=0.4)
+            nc.scalar.activation(q[:, c], a2[:, c], ACT.Abs_reciprocal_sqrt, bias=1.0)
+            return q
+
+        def finish(b, dth, q, t0, t1):
+            c = tile_cols(t0, t1)
+            turn, num, res = [held("%s%d%d" % (n, b, t0), [P, S], F32) for n in ("turn", "num", "res")]
+            nc.vector.scalar_tensor_tensor(turn[:, c], dth[:, c], 0.4, nsn[b][:, c], MULT, MULT)
+            nc.vector.tensor_tensor(num[:, c], turn[:, c], cs[b][:, c], ADD)
+            nc.vector.tensor_tensor(res[:, c], num[:, c], q[:, c], MULT)
+            nc.sync.dma_start(out[b * P : (b + 1) * P, c], res[:, c])
+
+        turn_cpl()
+        for o in range(PASSES):
+            for i in range(2):
+                grouped = held("grouped0%d%d" % (i, o), [P, P, PACK], BF16)
+                interleave(grouped[:], 0, i, o, nc.vector.tensor_copy if o == PASSES - 1 else nc.scalar.copy)
+                quantise("0%d%d" % (i, o), grouped[:], [(0, i, o)])
+        yz = products(0, ("B1", "B7"))
+        normalise(0, *yz, radius(0, *yz))
+        for o, tag in enumerate(("r20", "rinv0")):
+            grouped = shared(tag, "grouped1%d" % o, [P, 2 * P, PACK], BF16)
+            for i in range(2):
+                interleave(grouped[:, i * P : (i + 1) * P, :], 1, i, o, nc.scalar.copy)
+            quantise("1%d" % o, grouped[:], [(1, 0, o), (1, 1, o)])
+        yz = products(1, ("B1",))
+        rinv1 = radius(1, *yz)
+
+        f = [[held("f%d%d" % (b, d), [P, S], F32) for d in range(D)] for b in range(BLOCKS)]
+        v0 = held("v00", [P, S], F32)
+        x0 = shared("r20", "x00", [P, S], F32)
+        vx1 = shared("rinv0", "vx01", [P, 2, S], F32)
+        v2 = held("v02", [P, S], F32)
+        x2 = shared("sq11", "x02", [P, S], F32)
+        pairs = [(v0[:], x0[:]), (vx1[:, 0, :], vx1[:, 1, :]), (v2[:], x2[:])]
+        for d, (v, x) in enumerate(pairs):
+            neighbour(0, d, v, x)
+        normalise(1, *yz, rinv1)
+        dth0 = bank("B6", "dth0")
+        add_turned(dth0, [turn_freq(0, "sq10")] + f[0], 0, TILES, opens=True, closes=True)
+        q0 = damping(0, dth0, 0, TILES)
+        freq_t1 = turn_freq(1, "rinv1")
+
+        v = [held("v1%d" % d, [P, S], F32) for d in range(D)]
+        x = [held("x1%d" % d, [P, S], F32) for d in range(D)]
+        halves = [(0, 2), (2, 4)]
+        dth1 = [bank(tag, "dth1" + tag) for tag in ("B0", "B1")]
+        last = [bank(tag, "cross12" + tag) for tag in ("B4", "B5")]
+        neighbour(1, 0, v[0][:], x[0][:])
+        cross = bank("B3", "cross11")
+        gather_sn(1, 1, v[1][:])
+        add_turned(cross, [v[1]], 0, TILES, opens=True)
+        for h, half in enumerate(halves):
+            add_turned(dth1[h], [freq_t1, f[1][0]], *half, opens=True)
+        gather_cs(1, 1, x[1], 0, TILES)
+        add_turned(cross, [x[1]], 0, TILES, closes=True)
+        weigh(1, f[1][1], cross, 0, TILES)
+        gather_sn(1, 2, v[2][:])
+        for h, half in enumerate(halves):
+            add_turned(last[h], [v[2]], *half, opens=True)
+        for h, half in enumerate(halves):
+            gather_cs(1, 2, x[2], *half)
+            add_turned(last[h], [x[2]], *half, closes=True)
+            weigh(2, f[1][2], last[h], *half)
+            if h == 0:
+                for g, other in enumerate(halves):
+                    add_turned(dth1[g], [f[1][1]], *other)
+        for h, half in enumerate(halves):
+            add_turned(dth1[h], [f[1][2]], *half, closes=True)
+        finish(0, dth0, q0, 0, TILES)
+        for h, half in enumerate(halves):
+            finish(1, dth1[h], damping(1, dth1[h], *half), *half)

@@ -11,6 +11,8 @@ PASSES = K // K_PASS
 BLOCKS = N // P
 TILES = S // P
 SPARE = 8
+HALVES = ((0, 2), (2, 4))
+HALF_COLS = (slice(0, S // 2), slice(S // 2, S))
 FLOPS = 2 * 2 * K * N * S
 
 F32 = mybir.dt.float32
@@ -34,7 +36,7 @@ def tile_picked_yphas_step_p_kernel(
         psum = ctx.enter_context(tc.psum_pool(name="psum", bufs=1))
 
         def held(name, shape, dtype):
-            return keep.tile(shape, dtype, name=name, align_bytes=64)
+            return keep.tile(shape, dtype, name=name, tag=name, align_bytes=64)
 
         x_tab = [held("x_tab%d" % o, [P, T], I32) for o in range(PASSES)]
         s_tab = held("s_tab", [P, T], U8)
@@ -73,14 +75,15 @@ def tile_picked_yphas_step_p_kernel(
         for o in range(PASSES):
             for i in range(2):
                 load_w(0, i, o)
+        for i in range(2):
+            load_w(1, i, 0)
         nc.sync.dma_start(cpl_rows[0:TILES, :, :], cpl[:, 0, :].rearrange("d (t p) -> t d p", p=P))
-        for o in range(PASSES):
-            for i in range(2):
-                load_w(1, i, o)
         for d, pos in enumerate((pos1, pos2, pos3)):
             nc.sync.dma_start(pos_sb[d][:], pos)
         for b in range(BLOCKS):
             nc.sync.dma_start(freq_sb[b][:], freq[b * P : (b + 1) * P, :])
+        for i in range(2):
+            load_w(1, i, 1)
 
         def shared(tag, name, shape, dtype):
             return keep.tile(shape, dtype, name=name, tag=tag, align_bytes=64)
@@ -96,18 +99,20 @@ def tile_picked_yphas_step_p_kernel(
 
         w_codes, w_bytes = {}, {}
 
-        def interleave(grouped, b, i, o, copy):
-            copy(
-                grouped.rearrange("p (c n) j -> p c j n", n=4),
-                w_raw[b, i, o][:].rearrange("p j (c n) -> p c j n", n=4),
-            )
+        def interleave(grouped, raw, copy):
+            copy(grouped.rearrange("p (c n) j -> p c j n", n=4), raw.rearrange("p j (c n) -> p c j n", n=4))
 
-        def quantise(name, grouped, keys):
+        def quantise(name, grouped, keys, pieces):
             codes = held("w_codes" + name, [P, len(keys) * P], U32)
             planes = held("w_bytes" + name, [P, len(keys) * P], U8)
-            nc.vector.quantize_mx(
-                out=codes[:].bitcast(FP8X4), scales=planes[:], in_=grouped.rearrange("p n j -> p (n j)")
-            )
+            width = len(keys) * P // pieces
+            for h in range(pieces):
+                c = slice(h * width, (h + 1) * width)
+                nc.vector.quantize_mx(
+                    out=codes[:, c].bitcast(FP8X4),
+                    scales=planes[:, c],
+                    in_=grouped[:, c, :].rearrange("p n j -> p (n j)"),
+                )
             for n, key in enumerate(keys):
                 w_codes[key] = codes[:, n * P : (n + 1) * P]
                 w_bytes[key] = planes[:, n * P : (n + 1) * P]
@@ -152,8 +157,9 @@ def tile_picked_yphas_step_p_kernel(
             return rinv
 
         def normalise(b, y, z, cuts, rinv):
-            for zh, c in zip(z, cuts):
-                nc.vector.tensor_tensor(sn[b][:, c], zh[:, c], rinv[:, c], MULT)
+            for h, c in enumerate(HALF_COLS):
+                if h < len(z):
+                    nc.vector.tensor_tensor(sn[b][:, cuts[h]], z[h][:, cuts[h]], rinv[:, cuts[h]], MULT)
                 nc.vector.tensor_tensor(cs[b][:, c], y[:, c], rinv[:, c], MULT)
             nc.scalar.activation(nsn[b][:], sn[b][:, :S], ACT.Copy, scale=-1.0)
 
@@ -165,11 +171,14 @@ def tile_picked_yphas_step_p_kernel(
                 nc.tensor.transpose(turned[:, d * P : (d + 1) * P], cpl_rows[:, d, :], ident[:])
             nc.scalar.copy(cpl_t[:], turned[:].rearrange("p (d r) -> p d r", r=P)[:, 0:D, 0:TILES])
 
-        def turn_freq(b, tag):
-            turned = bank("B5", "freq_turned%d" % b)
+        def turn_freq(b):
+            turned = bank("B%d" % (5 + b), "freq_turned%d" % b)
             for t in range(TILES):
                 nc.tensor.transpose(turned[:, t * P : (t + 1) * P], freq_sb[b][:, t * P : (t + 1) * P], ident[:])
-            freq_t = shared(tag, "freq_t%d" % b, [P, S], F32)
+            return turned
+
+        def keep_freq(b, turned):
+            freq_t = shared("w_raw1%d1" % (1 - b), "freq_t%d" % b, [P, S], F32)
             nc.scalar.copy(freq_t[:], turned[:])
             return freq_t
 
@@ -185,7 +194,10 @@ def tile_picked_yphas_step_p_kernel(
                 )
 
         def gather_sn(b, d, v):
-            nc.vector.tensor_tensor(v, sn[b][:].indirect(pos_sb[d][:]), cs[b][:, :S], MULT)
+            for t0, t1 in HALVES if d == 0 else [(0, TILES)]:
+                places = pos_sb[d][:, t0 * P // 16 : t1 * P // 16]
+                c = tile_cols(t0, t1)
+                nc.vector.tensor_tensor(v[:, c], sn[b][:].indirect(places), cs[b][:, c], MULT)
 
         def gather_cs(b, d, x, t0, t1):
             places = pos_sb[d][:, t0 * P // 16 : t1 * P // 16]
@@ -204,63 +216,81 @@ def tile_picked_yphas_step_p_kernel(
             add_turned(cross, [x], 0, TILES, closes=True)
             weigh(d, f[b][d], cross, 0, TILES)
 
-        def damping(b, dth, t0, t1):
-            c = tile_cols(t0, t1)
-            a2, q = [held("%s%d%d" % (n, b, t0), [P, S], F32) for n in ("a2", "q")]
-            nc.scalar.activation(a2[:, c], dth[:, c], ACT.Square, scale=0.4)
-            nc.scalar.activation(q[:, c], a2[:, c], ACT.Abs_reciprocal_sqrt, bias=1.0)
+        def damping(b, dth, cuts):
+            a2, q = [held("%s%d" % (n, b), [P, S], F32) for n in ("a2", "q")]
+            for acc, c in zip(dth, cuts):
+                nc.scalar.activation(a2[:, c], acc[:, c], ACT.Square, scale=0.4)
+            for c in cuts:
+                nc.scalar.activation(q[:, c], a2[:, c], ACT.Abs_reciprocal_sqrt, bias=1.0)
             return q
 
-        def finish(b, dth, q, t0, t1):
-            c = tile_cols(t0, t1)
-            turn, num, res = [held("%s%d%d" % (n, b, t0), [P, S], F32) for n in ("turn", "num", "res")]
-            nc.vector.scalar_tensor_tensor(turn[:, c], dth[:, c], 0.4, nsn[b][:, c], MULT, MULT)
-            nc.vector.tensor_tensor(num[:, c], turn[:, c], cs[b][:, c], ADD)
-            nc.vector.tensor_tensor(res[:, c], num[:, c], q[:, c], MULT)
-            nc.sync.dma_start(out[b * P : (b + 1) * P, c], res[:, c])
+        def finish(b, dth, q):
+            turn, num = [held("%s%d" % (n, b), [P, S], F32) for n in ("turn", "num")]
+            res = [held("res%d%d" % (b, h), [P, S // 2], F32) for h in range(2)]
+            for acc, c in zip(dth, HALF_COLS):
+                nc.vector.scalar_tensor_tensor(turn[:, c], acc[:, c], 0.4, nsn[b][:, c], MULT, MULT)
+            for c in HALF_COLS:
+                nc.vector.tensor_tensor(num[:, c], turn[:, c], cs[b][:, c], ADD)
+            for h, c in enumerate(HALF_COLS):
+                nc.vector.tensor_tensor(res[h][:], num[:, c], q[:, c], MULT)
+                nc.sync.dma_start(out[b * P : (b + 1) * P, c], res[h][:])
 
-        turn_cpl()
         for o in range(PASSES):
             for i in range(2):
                 grouped = held("grouped0%d%d" % (i, o), [P, P, PACK], BF16)
-                interleave(grouped[:], 0, i, o, nc.vector.tensor_copy if o == PASSES - 1 else nc.scalar.copy)
-                quantise("0%d%d" % (i, o), grouped[:], [(0, i, o)])
+                if o == 0:
+                    interleave(grouped[:], w_raw[0, i, o][:], nc.scalar.copy)
+                    quantise("0%d%d" % (i, o), grouped[:], [(0, i, o)], 1)
+                else:
+                    for c in (slice(0, P // 2), slice(P // 2, P)):
+                        interleave(grouped[:, c, :], w_raw[0, i, o][:, :, c], nc.vector.tensor_copy)
+                    quantise("0%d%d" % (i, o), grouped[:], [(0, i, o)], 2)
         yz = products(0, ("B1", "B7"))
         normalise(0, *yz, radius(0, *yz))
+        turn_cpl()
+        turned = [turn_freq(b) for b in range(BLOCKS)]
         for o, tag in enumerate(("r20", "rinv0")):
             grouped = shared(tag, "grouped1%d" % o, [P, 2 * P, PACK], BF16)
             for i in range(2):
-                interleave(grouped[:, i * P : (i + 1) * P, :], 1, i, o, nc.scalar.copy)
-            quantise("1%d" % o, grouped[:], [(1, 0, o), (1, 1, o)])
+                interleave(grouped[:, i * P : (i + 1) * P, :], w_raw[1, i, o][:], nc.scalar.copy)
+            quantise("1%d" % o, grouped[:], [(1, 0, o), (1, 1, o)], 1)
+        freq_t = [keep_freq(b, turned[b]) for b in range(BLOCKS)]
         yz = products(1, ("B1",))
         rinv1 = radius(1, *yz)
 
         f = [[held("f%d%d" % (b, d), [P, S], F32) for d in range(D)] for b in range(BLOCKS)]
         v0 = held("v00", [P, S], F32)
         x0 = shared("r20", "x00", [P, S], F32)
-        vx1 = shared("rinv0", "vx01", [P, 2, S], F32)
-        v2 = held("v02", [P, S], F32)
+        late = shared("rinv0", "late0", [P, 3, S], F32)
         x2 = shared("sq11", "x02", [P, S], F32)
-        pairs = [(v0[:], x0[:]), (vx1[:, 0, :], vx1[:, 1, :]), (v2[:], x2[:])]
-        for d, (v, x) in enumerate(pairs):
-            neighbour(0, d, v, x)
+        dth0 = bank("B7", "dth0")
+        halves = [(0, 2), (2, 4)]
+        neighbour(0, 0, v0[:], x0[:])
+        neighbour(0, 1, late[:, 0, :], late[:, 1, :])
+        add_turned(dth0, [freq_t[0], f[0][0]], 0, TILES, opens=True)
+        cross = bank("B4", "cross02")
+        gather_sn(0, 2, late[:, 2, :])
+        add_turned(cross, [late[:, 2, :]], 0, TILES, opens=True)
+        add_turned(dth0, [f[0][1]], 0, TILES)
+        gather_cs(0, 2, x2, 0, TILES)
+        add_turned(cross, [x2], 0, TILES, closes=True)
         normalise(1, *yz, rinv1)
-        dth0 = bank("B6", "dth0")
-        add_turned(dth0, [turn_freq(0, "sq10")] + f[0], 0, TILES, opens=True, closes=True)
-        q0 = damping(0, dth0, 0, TILES)
-        freq_t1 = turn_freq(1, "rinv1")
+        weigh(2, f[0][2], cross, 0, TILES)
+        dth1 = [bank(tag, "dth1" + tag) for tag in ("B5", "B6")]
+        for h, half in enumerate(halves):
+            add_turned(dth1[h], [freq_t[1]], *half, opens=True)
+        add_turned(dth0, [f[0][2]], 0, TILES, closes=True)
+        q0 = damping(0, [dth0], [slice(0, S)])
 
         v = [held("v1%d" % d, [P, S], F32) for d in range(D)]
         x = [held("x1%d" % d, [P, S], F32) for d in range(D)]
-        halves = [(0, 2), (2, 4)]
-        dth1 = [bank(tag, "dth1" + tag) for tag in ("B0", "B1")]
-        last = [bank(tag, "cross12" + tag) for tag in ("B4", "B5")]
+        last = [bank(tag, "cross12" + tag) for tag in ("B0", "B1")]
         neighbour(1, 0, v[0][:], x[0][:])
         cross = bank("B3", "cross11")
         gather_sn(1, 1, v[1][:])
         add_turned(cross, [v[1]], 0, TILES, opens=True)
         for h, half in enumerate(halves):
-            add_turned(dth1[h], [freq_t1, f[1][0]], *half, opens=True)
+            add_turned(dth1[h], [f[1][0]], *half)
         gather_cs(1, 1, x[1], 0, TILES)
         add_turned(cross, [x[1]], 0, TILES, closes=True)
         weigh(1, f[1][1], cross, 0, TILES)
@@ -271,11 +301,8 @@ def tile_picked_yphas_step_p_kernel(
             gather_cs(1, 2, x[2], *half)
             add_turned(last[h], [x[2]], *half, closes=True)
             weigh(2, f[1][2], last[h], *half)
-            if h == 0:
-                for g, other in enumerate(halves):
-                    add_turned(dth1[g], [f[1][1]], *other)
+            add_turned(dth1[h], [f[1][1]], *half)
         for h, half in enumerate(halves):
             add_turned(dth1[h], [f[1][2]], *half, closes=True)
-        finish(0, dth0, q0, 0, TILES)
-        for h, half in enumerate(halves):
-            finish(1, dth1[h], damping(1, dth1[h], *half), *half)
+        finish(0, [dth0, dth0], q0)
+        finish(1, dth1, damping(1, dth1, HALF_COLS))

@@ -64,26 +64,27 @@ def tile_picked_yphas_step_p_kernel(
             rows = (w1, w2)[i][o * K_PASS : (o + 1) * K_PASS, b * P : (b + 1) * P]
             nc.sync.dma_start(w_raw[b, i, o][:], rows.rearrange("(p j) n -> p j n", j=PACK))
 
-        load_x(0)
         nc.sync.dma_start(offs_sb[:], offs)
+        load_x(0)
         for q in range(4):
             nc.sync.dma_start(
                 s_tab[32 * q : 32 * q + 4 * PASSES, :].bitcast(I32),
                 x_scales[:, 4 * q : 4 * q + 4, :].bitcast(I32),
             )
+        for i in range(2):
+            load_w(0, i, 0)
         load_x(1)
-        for o in range(PASSES):
-            for i in range(2):
-                load_w(0, i, o)
+        for i in range(2):
+            load_w(0, i, 1)
         for i in range(2):
             load_w(1, i, 0)
         nc.sync.dma_start(cpl_rows[0:TILES, :, :], cpl[:, 0, :].rearrange("d (t p) -> t d p", p=P))
+        for i in range(2):
+            load_w(1, i, 1)
         for d, pos in enumerate((pos1, pos2, pos3)):
             nc.sync.dma_start(pos_sb[d][:], pos)
         for b in range(BLOCKS):
             nc.sync.dma_start(freq_sb[b][:], freq[b * P : (b + 1) * P, :])
-        for i in range(2):
-            load_w(1, i, 1)
 
         def shared(tag, name, shape, dtype):
             return keep.tile(shape, dtype, name=name, tag=tag, align_bytes=64)
@@ -124,43 +125,51 @@ def tile_picked_yphas_step_p_kernel(
             nc.gpsimd.memset(cs[b][:, S:], 0.0)
             nc.gpsimd.memset(sn[b][:, S:], 0.0)
 
-        def products(b, z_tags):
-            width = S // len(z_tags)
-            cuts = [slice(h * width, (h + 1) * width) for h in range(len(z_tags))]
-            y = bank("B0", "y%d" % b)
-            z = [bank(tag, "z%d%s" % (b, tag)) for tag in z_tags]
-            groups = [(0, y, slice(0, S))] + [(1, zh, c) for zh, c in zip(z, cuts)]
+        def products(b, tags):
+            pieces = len(tags) // 2
+            width = S // pieces
+            cuts = [slice(h * width, (h + 1) * width) for h in range(pieces)]
+            yz = [[bank(tags[i * pieces + h], "yz%d%d%d" % (b, i, h)) for h in range(pieces)] for i in range(2)]
             for o in range(PASSES):
-                for i, acc, c in groups:
-                    nc.tensor.matmul_mx(
-                        out=acc[:, c],
-                        lhsT=w_codes[b, i, o].bitcast(FP8X4),
-                        lhsT_scale=w_bytes[b, i, o],
-                        rhs=x_codes[o][:, c].bitcast(FP8X4),
-                        rhs_scale=x_bytes[4 * o :, c],
-                        start=(o == 0),
-                        stop=(o == PASSES - 1),
-                    )
-            return y, z, cuts
+                for i in range(2):
+                    for acc, c in zip(yz[i], cuts):
+                        nc.tensor.matmul_mx(
+                            out=acc[:, c],
+                            lhsT=w_codes[b, i, o].bitcast(FP8X4),
+                            lhsT_scale=w_bytes[b, i, o],
+                            rhs=x_codes[o][:, c].bitcast(FP8X4),
+                            rhs_scale=x_bytes[4 * o :, c],
+                            start=(o == 0),
+                            stop=(o == PASSES - 1),
+                        )
+            return yz[0], yz[1], cuts
 
         def radius(b, y, z, cuts):
             sq = [shared("sq%d%d" % (b, i), "sq%d%d" % (b, i), [P, S], F32) for i in range(2)]
             r2 = shared("r2%d" % b, "r2%d" % b, [P, S], F32)
             rinv = shared("rinv%d" % b, "rinv%d" % b, [P, S], F32)
-            nc.scalar.activation(sq[0][:], y[:], ACT.Square)
-            for zh, c in zip(z, cuts):
-                nc.scalar.activation(sq[1][:, c], zh[:, c], ACT.Square)
+            for i, accs in enumerate((y, z)):
+                for acc, c in zip(accs, cuts):
+                    nc.scalar.activation(sq[i][:, c], acc[:, c], ACT.Square)
+            if b == 0:
+                for c in cuts:
+                    nc.vector.tensor_tensor(r2[:, c], sq[0][:, c], sq[1][:, c], ADD)
+                total = r2
+            else:
+                turned_sum = bank("B4", "r2_turned")
+                add_turned(turned_sum, sq, 0, TILES, opens=True, closes=True)
+                nc.scalar.copy(r2[:], turned_sum[:])
+                total = bank("B7", "r2_back")
+                add_turned(total, [r2], 0, TILES, opens=True, closes=True)
             for c in cuts:
-                nc.vector.tensor_tensor(r2[:, c], sq[0][:, c], sq[1][:, c], ADD)
-            for c in cuts:
-                nc.scalar.activation(rinv[:, c], r2[:, c], ACT.Abs_reciprocal_sqrt, bias=0.1)
+                nc.scalar.activation(rinv[:, c], total[:, c], ACT.Abs_reciprocal_sqrt, bias=0.1)
             return rinv
 
         def normalise(b, y, z, cuts, rinv):
             for h, c in enumerate(HALF_COLS):
                 if h < len(z):
                     nc.vector.tensor_tensor(sn[b][:, cuts[h]], z[h][:, cuts[h]], rinv[:, cuts[h]], MULT)
-                nc.vector.tensor_tensor(cs[b][:, c], y[:, c], rinv[:, c], MULT)
+                nc.vector.tensor_tensor(cs[b][:, c], y[h % len(y)][:, c], rinv[:, c], MULT)
             nc.scalar.activation(nsn[b][:], sn[b][:, :S], ACT.Copy, scale=-1.0)
 
         cpl_t = held("cpl_t", [P, D, TILES], F32)
@@ -238,40 +247,44 @@ def tile_picked_yphas_step_p_kernel(
         for o in range(PASSES):
             for i in range(2):
                 grouped = held("grouped0%d%d" % (i, o), [P, P, PACK], BF16)
-                if o == 0:
+                if (o, i) != (PASSES - 1, 1):
                     interleave(grouped[:], w_raw[0, i, o][:], nc.scalar.copy)
                     quantise("0%d%d" % (i, o), grouped[:], [(0, i, o)], 1)
                 else:
-                    for c in (slice(0, P // 2), slice(P // 2, P)):
-                        interleave(grouped[:, c, :], w_raw[0, i, o][:, :, c], nc.vector.tensor_copy)
+                    for c, copy in ((slice(0, P // 2), nc.vector.tensor_copy), (slice(P // 2, P), nc.scalar.copy)):
+                        interleave(grouped[:, c, :], w_raw[0, i, o][:, :, c], copy)
                     quantise("0%d%d" % (i, o), grouped[:], [(0, i, o)], 2)
-        yz = products(0, ("B1", "B7"))
+        yz = products(0, ("B0", "B2", "B1", "B7"))
         normalise(0, *yz, radius(0, *yz))
         turn_cpl()
         turned = [turn_freq(b) for b in range(BLOCKS)]
-        for o, tag in enumerate(("r20", "rinv0")):
-            grouped = shared(tag, "grouped1%d" % o, [P, 2 * P, PACK], BF16)
-            for i in range(2):
-                interleave(grouped[:, i * P : (i + 1) * P, :], w_raw[1, i, o][:], nc.scalar.copy)
-            quantise("1%d" % o, grouped[:], [(1, 0, o), (1, 1, o)], 1)
+        grouped = [held("grouped1%d0" % i, [P, P, PACK], BF16) for i in range(2)]
+        for i in range(2):
+            interleave(grouped[i][:], w_raw[1, i, 0][:], nc.vector.tensor_copy)
+        for i in range(2):
+            quantise("1%d0" % i, grouped[i][:], [(1, i, 0)], 1)
+        grouped = shared("r20", "grouped11", [P, 2 * P, PACK], BF16)
+        for i in range(2):
+            interleave(grouped[:, i * P : (i + 1) * P, :], w_raw[1, i, 1][:], nc.scalar.copy)
+        quantise("11", grouped[:], [(1, 0, 1), (1, 1, 1)], 1)
         freq_t = [keep_freq(b, turned[b]) for b in range(BLOCKS)]
-        yz = products(1, ("B1",))
+        yz = products(1, ("B0", "B1"))
         rinv1 = radius(1, *yz)
 
         f = [[held("f%d%d" % (b, d), [P, S], F32) for d in range(D)] for b in range(BLOCKS)]
         v0 = held("v00", [P, S], F32)
-        x0 = shared("r20", "x00", [P, S], F32)
-        late = shared("rinv0", "late0", [P, 3, S], F32)
-        x2 = shared("sq11", "x02", [P, S], F32)
+        late = shared("r20", "late0", [P, 5, S], F32)
+        v2 = late[:, 3, :]
         dth0 = bank("B7", "dth0")
         halves = [(0, 2), (2, 4)]
-        neighbour(0, 0, v0[:], x0[:])
-        neighbour(0, 1, late[:, 0, :], late[:, 1, :])
+        neighbour(0, 0, v0[:], late[:, 0, :])
+        neighbour(0, 1, late[:, 1, :], late[:, 2, :])
         add_turned(dth0, [freq_t[0], f[0][0]], 0, TILES, opens=True)
         cross = bank("B4", "cross02")
-        gather_sn(0, 2, late[:, 2, :])
-        add_turned(cross, [late[:, 2, :]], 0, TILES, opens=True)
+        gather_sn(0, 2, v2)
+        add_turned(cross, [v2], 0, TILES, opens=True)
         add_turned(dth0, [f[0][1]], 0, TILES)
+        x2 = late[:, 4, :]
         gather_cs(0, 2, x2, 0, TILES)
         add_turned(cross, [x2], 0, TILES, closes=True)
         normalise(1, *yz, rinv1)

@@ -10,9 +10,13 @@ K_PASS = P * PACK
 PASSES = K // K_PASS
 BLOCKS = N // P
 TILES = S // P
+QUADRANT = 32
+SCALE_ROWS = 4
+GROUP = 16
+LINE = 4
 SPARE = 8
-HALVES = ((0, 2), (2, 4))
-HALF_COLS = (slice(0, S // 2), slice(S // 2, S))
+WHOLE = (0, TILES)
+HALVES = ((0, TILES // 2), (TILES // 2, TILES))
 FLOPS = 2 * 2 * K * N * S
 
 F32 = mybir.dt.float32
@@ -27,6 +31,10 @@ MULT = mybir.AluOpType.mult
 ADD = mybir.AluOpType.add
 
 
+def cols(part):
+    return slice(part[0] * P, part[1] * P)
+
+
 def tile_picked_yphas_step_p_kernel(
     tc, x_words, x_scales, w1, w2, cpl, freq, offs, pos1, pos2, pos3, out
 ):
@@ -35,13 +43,16 @@ def tile_picked_yphas_step_p_kernel(
         keep = ctx.enter_context(tc.tile_pool(name="keep", bufs=1))
         psum = ctx.enter_context(tc.psum_pool(name="psum", bufs=1))
 
-        def held(name, shape, dtype):
-            return keep.tile(shape, dtype, name=name, tag=name, align_bytes=64)
+        def held(name, shape, dtype, on=None):
+            return keep.tile(shape, dtype, name=name, tag=on or name, align_bytes=64)
+
+        def bank(number, name):
+            return psum.tile([P, S], F32, name=name, tag="bank%d" % number)
 
         x_tab = [held("x_tab%d" % o, [P, T], I32) for o in range(PASSES)]
         s_tab = held("s_tab", [P, T], U8)
-        offs_sb = held("offs_sb", [P, S // 16], U16)
-        pos_sb = [held("pos_sb%d" % d, [P, S // 16], U16) for d in range(D)]
+        offs_sb = held("offs_sb", [P, S // GROUP], U16)
+        pos_sb = [held("pos_sb%d" % d, [P, S // GROUP], U16) for d in range(D)]
         w_raw = {
             (b, i, o): held("w_raw%d%d%d" % (b, i, o), [P, PACK, P], F32)
             for b in range(BLOCKS) for i in range(2) for o in range(PASSES)
@@ -49,48 +60,41 @@ def tile_picked_yphas_step_p_kernel(
         freq_sb = [held("freq_sb%d" % b, [P, S], F32) for b in range(BLOCKS)]
         cpl_rows = held("cpl_rows", [P, D, P], F32)
         ident = held("ident", [P, P], F32)
-        warm = held("warm", [P, 8], F32)
 
         nc.vector.memset(s_tab[:].bitcast(I32), 0)
-        nc.vector.memset(warm[:], 1.0)
-        nc.scalar.activation(warm[:, 0:1], warm[:, 1:2], ACT.Abs_reciprocal_sqrt)
+        cs = [held("cs%d" % b, [P, S + SPARE], F32) for b in range(BLOCKS)]
+        sn = [held("sn%d" % b, [P, S + SPARE], F32) for b in range(BLOCKS)]
+        nc.vector.memset(cs[0][:, S:], 1.0)
+        for window in (sn[0], cs[1], sn[1]):
+            nc.scalar.activation(window[:, S:], cs[0][:, S:], ACT.Abs_reciprocal_sqrt)
         make_identity(nc, ident[:])
         nc.gpsimd.memset(cpl_rows[:], 0.0)
 
         def load_x(o):
             nc.sync.dma_start(x_tab[o][:], x_words[o].rearrange("p c r -> p (c r)").bitcast(I32))
 
-        def load_w(b, i, o):
-            rows = (w1, w2)[i][o * K_PASS : (o + 1) * K_PASS, b * P : (b + 1) * P]
-            nc.sync.dma_start(w_raw[b, i, o][:], rows.rearrange("(p j) n -> p j n", j=PACK))
+        def load_w(b, o):
+            for i, w in enumerate((w1, w2)):
+                rows = w[o * K_PASS : (o + 1) * K_PASS, b * P : (b + 1) * P]
+                nc.sync.dma_start(w_raw[b, i, o][:], rows.rearrange("(p j) n -> p j n", j=PACK))
 
         nc.sync.dma_start(offs_sb[:], offs)
         load_x(0)
-        for q in range(4):
+        for q in range(P // QUADRANT):
             nc.sync.dma_start(
-                s_tab[32 * q : 32 * q + 4 * PASSES, :].bitcast(I32),
-                x_scales[:, 4 * q : 4 * q + 4, :].bitcast(I32),
+                s_tab[QUADRANT * q : QUADRANT * q + SCALE_ROWS * PASSES, :].bitcast(I32),
+                x_scales[:, SCALE_ROWS * q : SCALE_ROWS * (q + 1), :].bitcast(I32),
             )
-        for i in range(2):
-            load_w(0, i, 0)
+        load_w(0, 0)
         load_x(1)
-        for i in range(2):
-            load_w(0, i, 1)
-        for i in range(2):
-            load_w(1, i, 0)
+        load_w(0, 1)
+        load_w(1, 0)
         nc.sync.dma_start(cpl_rows[0:TILES, :, :], cpl[:, 0, :].rearrange("d (t p) -> t d p", p=P))
-        for i in range(2):
-            load_w(1, i, 1)
+        load_w(1, 1)
         for d, pos in enumerate((pos1, pos2, pos3)):
             nc.sync.dma_start(pos_sb[d][:], pos)
         for b in range(BLOCKS):
             nc.sync.dma_start(freq_sb[b][:], freq[b * P : (b + 1) * P, :])
-
-        def shared(tag, name, shape, dtype):
-            return keep.tile(shape, dtype, name=name, tag=tag, align_bytes=64)
-
-        def bank(tag, name):
-            return psum.tile([P, S], F32, name=name, tag=tag)
 
         x_codes = [held("x_codes%d" % o, [P, S], U32) for o in range(PASSES)]
         x_bytes = held("x_bytes", [P, S], U8)
@@ -101,147 +105,117 @@ def tile_picked_yphas_step_p_kernel(
         w_codes, w_bytes = {}, {}
 
         def interleave(grouped, raw, copy):
-            copy(grouped.rearrange("p (c n) j -> p c j n", n=4), raw.rearrange("p j (c n) -> p c j n", n=4))
+            copy(grouped.rearrange("p (c n) j -> p c j n", n=LINE), raw.rearrange("p j (c n) -> p c j n", n=LINE))
 
-        def quantise(name, grouped, keys, pieces):
+        def quantise(grouped, keys, pieces=1):
+            name = "%d%d%d" % keys[0]
             codes = held("w_codes" + name, [P, len(keys) * P], U32)
-            planes = held("w_bytes" + name, [P, len(keys) * P], U8)
+            scales = held("w_bytes" + name, [P, len(keys) * P], U8)
             width = len(keys) * P // pieces
             for h in range(pieces):
                 c = slice(h * width, (h + 1) * width)
                 nc.vector.quantize_mx(
                     out=codes[:, c].bitcast(FP8X4),
-                    scales=planes[:, c],
+                    scales=scales[:, c],
                     in_=grouped[:, c, :].rearrange("p n j -> p (n j)"),
                 )
             for n, key in enumerate(keys):
                 w_codes[key] = codes[:, n * P : (n + 1) * P]
-                w_bytes[key] = planes[:, n * P : (n + 1) * P]
+                w_bytes[key] = scales[:, n * P : (n + 1) * P]
 
-        cs = [held("cs%d" % b, [P, S + SPARE], F32) for b in range(BLOCKS)]
-        sn = [held("sn%d" % b, [P, S + SPARE], F32) for b in range(BLOCKS)]
-        nsn = [held("nsn%d" % b, [P, S], F32) for b in range(BLOCKS)]
-        for b in range(BLOCKS):
-            nc.gpsimd.memset(cs[b][:, S:], 0.0)
-            nc.gpsimd.memset(sn[b][:, S:], 0.0)
+        minus_sn = [held("minus_sn%d" % b, [P, S], F32) for b in range(BLOCKS)]
 
-        def products(b, tags):
-            pieces = len(tags) // 2
-            width = S // pieces
-            cuts = [slice(h * width, (h + 1) * width) for h in range(pieces)]
-            yz = [[bank(tags[i * pieces + h], "yz%d%d%d" % (b, i, h)) for h in range(pieces)] for i in range(2)]
+        def products(b, parts, y_banks, z_banks):
+            yz = [
+                [bank(number, "yz%d%d_%d" % (b, i, number)) for number in banks]
+                for i, banks in enumerate((y_banks, z_banks))
+            ]
             for o in range(PASSES):
                 for i in range(2):
-                    for acc, c in zip(yz[i], cuts):
+                    for acc, part in zip(yz[i], parts):
                         nc.tensor.matmul_mx(
-                            out=acc[:, c],
+                            out=acc[:, cols(part)],
                             lhsT=w_codes[b, i, o].bitcast(FP8X4),
                             lhsT_scale=w_bytes[b, i, o],
-                            rhs=x_codes[o][:, c].bitcast(FP8X4),
-                            rhs_scale=x_bytes[4 * o :, c],
+                            rhs=x_codes[o][:, cols(part)].bitcast(FP8X4),
+                            rhs_scale=x_bytes[SCALE_ROWS * o :, cols(part)],
                             start=(o == 0),
                             stop=(o == PASSES - 1),
                         )
-            return yz[0], yz[1], cuts
+            return yz
 
-        def radius(b, y, z, cuts):
-            sq = [shared("sq%d%d" % (b, i), "sq%d%d" % (b, i), [P, S], F32) for i in range(2)]
-            r2 = shared("r2%d" % b, "r2%d" % b, [P, S], F32)
-            rinv = shared("rinv%d" % b, "rinv%d" % b, [P, S], F32)
-            for i, accs in enumerate((y, z)):
-                for acc, c in zip(accs, cuts):
-                    nc.scalar.activation(sq[i][:, c], acc[:, c], ACT.Square)
-            if b == 0:
-                for c in cuts:
-                    nc.vector.tensor_tensor(r2[:, c], sq[0][:, c], sq[1][:, c], ADD)
-                total = r2
-            else:
-                turned_sum = bank("B4", "r2_turned")
-                add_turned(turned_sum, sq, 0, TILES, opens=True, closes=True)
-                nc.scalar.copy(r2[:], turned_sum[:])
-                total = bank("B7", "r2_back")
-                add_turned(total, [r2], 0, TILES, opens=True, closes=True)
-            for c in cuts:
-                nc.scalar.activation(rinv[:, c], total[:, c], ACT.Abs_reciprocal_sqrt, bias=0.1)
-            return rinv
-
-        def normalise(b, y, z, cuts, rinv):
-            for h, c in enumerate(HALF_COLS):
-                if h < len(z):
-                    nc.vector.tensor_tensor(sn[b][:, cuts[h]], z[h][:, cuts[h]], rinv[:, cuts[h]], MULT)
-                nc.vector.tensor_tensor(cs[b][:, c], y[h % len(y)][:, c], rinv[:, c], MULT)
-            nc.scalar.activation(nsn[b][:], sn[b][:, :S], ACT.Copy, scale=-1.0)
-
-        cpl_t = held("cpl_t", [P, D, TILES], F32)
-
-        def turn_cpl():
-            turned = bank("B5", "cpl_turned")
-            for d in range(D):
-                nc.tensor.transpose(turned[:, d * P : (d + 1) * P], cpl_rows[:, d, :], ident[:])
-            nc.scalar.copy(cpl_t[:], turned[:].rearrange("p (d r) -> p d r", r=P)[:, 0:D, 0:TILES])
-
-        def turn_freq(b):
-            turned = bank("B%d" % (5 + b), "freq_turned%d" % b)
-            for t in range(TILES):
-                nc.tensor.transpose(turned[:, t * P : (t + 1) * P], freq_sb[b][:, t * P : (t + 1) * P], ident[:])
-            return turned
-
-        def keep_freq(b, turned):
-            freq_t = shared("w_raw1%d1" % (1 - b), "freq_t%d" % b, [P, S], F32)
-            nc.scalar.copy(freq_t[:], turned[:])
-            return freq_t
-
-        def tile_cols(t0, t1):
-            return slice(t0 * P, t1 * P)
-
-        def add_turned(dst, srcs, t0, t1, opens=False, closes=False):
-            steps = [(src, tile_cols(t, t + 1)) for src in srcs for t in range(t0, t1)]
+        def add_turned(dst, srcs, part, opens=False, closes=False):
+            steps = [(src, cols((t, t + 1))) for src in srcs for t in range(*part)]
             for n, (src, c) in enumerate(steps):
                 nc.tensor.matmul(
                     dst[:, c], lhsT=src[:, c], rhs=ident[:], is_transpose=True,
                     start=(opens and n == 0), stop=(closes and n == len(steps) - 1),
                 )
 
-        def gather_sn(b, d, v):
-            for t0, t1 in HALVES if d == 0 else [(0, TILES)]:
-                places = pos_sb[d][:, t0 * P // 16 : t1 * P // 16]
-                c = tile_cols(t0, t1)
-                nc.vector.tensor_tensor(v[:, c], sn[b][:].indirect(places), cs[b][:, c], MULT)
+        def squares(b, yz, parts):
+            sq = [held("sq%d%d" % (b, i), [P, S], F32) for i in range(2)]
+            r2 = held("r2_%d" % b, [P, S], F32)
+            rinv = held("rinv%d" % b, [P, S], F32)
+            for i in range(2):
+                for acc, part in zip(yz[i], parts):
+                    nc.scalar.activation(sq[i][:, cols(part)], acc[:, cols(part)], ACT.Square)
+            return sq, r2, rinv
 
-        def gather_cs(b, d, x, t0, t1):
-            places = pos_sb[d][:, t0 * P // 16 : t1 * P // 16]
-            nc.vector.tensor_tensor(x[:, tile_cols(t0, t1)], cs[b][:].indirect(places), nsn[b][:, tile_cols(t0, t1)], MULT)
+        def inverse_radius(rinv, total, parts):
+            for part in parts:
+                nc.scalar.activation(rinv[:, cols(part)], total[:, cols(part)], ACT.Abs_reciprocal_sqrt, bias=0.1)
 
-        def weigh(d, f, cross, t0, t1):
-            for t in range(t0, t1):
-                c = tile_cols(t, t + 1)
-                nc.scalar.activation(f[:, c], cross[:, c], ACT.Copy, scale=cpl_t[:, d, t : t + 1])
+        def scale_by(window, acc, rinv, part):
+            nc.vector.tensor_tensor(window[:, cols(part)], acc[:, cols(part)], rinv[:, cols(part)], MULT)
 
-        def neighbour(b, d, v, x):
-            cross = bank("B%d" % (2 + d), "cross%d%d" % (b, d))
-            gather_sn(b, d, v)
-            add_turned(cross, [v], 0, TILES, opens=True)
-            gather_cs(b, d, x, 0, TILES)
-            add_turned(cross, [x], 0, TILES, closes=True)
-            weigh(d, f[b][d], cross, 0, TILES)
+        def negate_sn(b):
+            nc.scalar.activation(minus_sn[b][:], sn[b][:, :S], ACT.Copy, scale=-1.0)
 
-        def damping(b, dth, cuts):
-            a2, q = [held("%s%d" % (n, b), [P, S], F32) for n in ("a2", "q")]
-            for acc, c in zip(dth, cuts):
-                nc.scalar.activation(a2[:, c], acc[:, c], ACT.Square, scale=0.4)
-            for c in cuts:
-                nc.scalar.activation(q[:, c], a2[:, c], ACT.Abs_reciprocal_sqrt, bias=1.0)
-            return q
+        def places(d, part):
+            return pos_sb[d][:, part[0] * P // GROUP : part[1] * P // GROUP]
 
-        def finish(b, dth, q):
-            turn, num = [held("%s%d" % (n, b), [P, S], F32) for n in ("turn", "num")]
+        def gather_sn(b, d, term, part):
+            nc.vector.tensor_tensor(term[:, cols(part)], sn[b][:].indirect(places(d, part)), cs[b][:, cols(part)], MULT)
+
+        def gather_cs(b, d, term, part):
+            nc.vector.tensor_tensor(
+                term[:, cols(part)], cs[b][:].indirect(places(d, part)), minus_sn[b][:, cols(part)], MULT
+            )
+
+        def weigh(b, d, cross, part):
+            for t in range(*part):
+                c = cols((t, t + 1))
+                nc.scalar.activation(weighted[b][d][:, c], cross[:, c], ACT.Copy, scale=cpl_t[:, d, t : t + 1])
+
+        def neighbour(b, d, sn_term, cs_term, sn_parts):
+            cross = bank(2 + d, "cross%d%d" % (b, d))
+            for part in sn_parts:
+                gather_sn(b, d, sn_term, part)
+            add_turned(cross, [sn_term], WHOLE, opens=True)
+            gather_cs(b, d, cs_term, WHOLE)
+            add_turned(cross, [cs_term], WHOLE, closes=True)
+            weigh(b, d, cross, WHOLE)
+
+        def damping(b, dth, parts):
+            a2, damp = [held("%s%d" % (name, b), [P, S], F32) for name in ("a2_", "damp")]
+            for acc, part in zip(dth, parts):
+                nc.scalar.activation(a2[:, cols(part)], acc[:, cols(part)], ACT.Square, scale=0.4)
+            for part in parts:
+                nc.scalar.activation(damp[:, cols(part)], a2[:, cols(part)], ACT.Abs_reciprocal_sqrt, bias=1.0)
+            return damp
+
+        def finish(b, dth, damp):
+            pull, num = [held("%s%d" % (name, b), [P, S], F32) for name in ("pull", "num")]
             res = [held("res%d%d" % (b, h), [P, S // 2], F32) for h in range(2)]
-            for acc, c in zip(dth, HALF_COLS):
-                nc.vector.scalar_tensor_tensor(turn[:, c], acc[:, c], 0.4, nsn[b][:, c], MULT, MULT)
-            for c in HALF_COLS:
-                nc.vector.tensor_tensor(num[:, c], turn[:, c], cs[b][:, c], ADD)
-            for h, c in enumerate(HALF_COLS):
-                nc.vector.tensor_tensor(res[h][:], num[:, c], q[:, c], MULT)
+            for acc, half in zip(dth, HALVES):
+                c = cols(half)
+                nc.vector.scalar_tensor_tensor(pull[:, c], acc[:, c], 0.4, minus_sn[b][:, c], MULT, MULT)
+            for half in HALVES:
+                c = cols(half)
+                nc.vector.tensor_tensor(num[:, c], pull[:, c], cs[b][:, c], ADD)
+            for h, half in enumerate(HALVES):
+                c = cols(half)
+                nc.vector.tensor_tensor(res[h][:], num[:, c], damp[:, c], MULT)
                 nc.sync.dma_start(out[b * P : (b + 1) * P, c], res[h][:])
 
         for o in range(PASSES):
@@ -249,73 +223,104 @@ def tile_picked_yphas_step_p_kernel(
                 grouped = held("grouped0%d%d" % (i, o), [P, P, PACK], BF16)
                 if (o, i) != (PASSES - 1, 1):
                     interleave(grouped[:], w_raw[0, i, o][:], nc.scalar.copy)
-                    quantise("0%d%d" % (i, o), grouped[:], [(0, i, o)], 1)
+                    quantise(grouped[:], [(0, i, o)])
                 else:
                     for c, copy in ((slice(0, P // 2), nc.vector.tensor_copy), (slice(P // 2, P), nc.scalar.copy)):
                         interleave(grouped[:, c, :], w_raw[0, i, o][:, :, c], copy)
-                    quantise("0%d%d" % (i, o), grouped[:], [(0, i, o)], 2)
-        yz = products(0, ("B0", "B2", "B1", "B7"))
-        normalise(0, *yz, radius(0, *yz))
-        turn_cpl()
-        turned = [turn_freq(b) for b in range(BLOCKS)]
+                    quantise(grouped[:], [(0, i, o)], pieces=2)
+        y, z = products(0, HALVES, (0, 2), (1, 7))
+        sq, r2, rinv = squares(0, (y, z), HALVES)
+        for half in HALVES:
+            nc.vector.tensor_tensor(r2[:, cols(half)], sq[0][:, cols(half)], sq[1][:, cols(half)], ADD)
+        inverse_radius(rinv, r2, HALVES)
+        for h, half in enumerate(HALVES):
+            scale_by(sn[0], z[h], rinv, half)
+            scale_by(cs[0], y[h], rinv, half)
+        negate_sn(0)
+
+        cpl_t = held("cpl_t", [P, D, TILES], F32)
+        cpl_bank = bank(5, "cpl_bank")
+        for d in range(D):
+            nc.tensor.transpose(cpl_bank[:, d * P : (d + 1) * P], cpl_rows[:, d, :], ident[:])
+        nc.scalar.copy(cpl_t[:], cpl_bank[:].rearrange("p (d r) -> p d r", r=P)[:, 0:D, 0:TILES])
+        freq_banks = []
+        for b in range(BLOCKS):
+            freq_banks.append(bank(5 + b, "freq_bank%d" % b))
+            for t in range(TILES):
+                c = cols((t, t + 1))
+                nc.tensor.transpose(freq_banks[b][:, c], freq_sb[b][:, c], ident[:])
+
         grouped = [held("grouped1%d0" % i, [P, P, PACK], BF16) for i in range(2)]
         for i in range(2):
             interleave(grouped[i][:], w_raw[1, i, 0][:], nc.vector.tensor_copy)
         for i in range(2):
-            quantise("1%d0" % i, grouped[i][:], [(1, i, 0)], 1)
-        grouped = shared("r20", "grouped11", [P, 2 * P, PACK], BF16)
+            quantise(grouped[i][:], [(1, i, 0)])
+        grouped = held("grouped1_1", [P, 2 * P, PACK], BF16, on="r2_0")
         for i in range(2):
             interleave(grouped[:, i * P : (i + 1) * P, :], w_raw[1, i, 1][:], nc.scalar.copy)
-        quantise("11", grouped[:], [(1, 0, 1), (1, 1, 1)], 1)
-        freq_t = [keep_freq(b, turned[b]) for b in range(BLOCKS)]
-        yz = products(1, ("B0", "B1"))
-        rinv1 = radius(1, *yz)
+        quantise(grouped[:], [(1, 0, 1), (1, 1, 1)])
+        freq_t = []
+        for b in range(BLOCKS):
+            freq_t.append(held("freq_t%d" % b, [P, S], F32, on="w_raw1%d1" % (1 - b)))
+            nc.scalar.copy(freq_t[b][:], freq_banks[b][:])
+        (y,), (z,) = products(1, [WHOLE], (0,), (1,))
+        sq, r2, rinv = squares(1, ([y], [z]), [WHOLE])
+        r2_turned = bank(4, "r2_turned")
+        add_turned(r2_turned, sq, WHOLE, opens=True, closes=True)
+        nc.scalar.copy(r2[:], r2_turned[:])
+        r2_back = bank(7, "r2_back")
+        add_turned(r2_back, [r2], WHOLE, opens=True, closes=True)
+        inverse_radius(rinv, r2_back, [WHOLE])
 
-        f = [[held("f%d%d" % (b, d), [P, S], F32) for d in range(D)] for b in range(BLOCKS)]
-        v0 = held("v00", [P, S], F32)
-        late = shared("r20", "late0", [P, 5, S], F32)
-        v2 = late[:, 3, :]
-        dth0 = bank("B7", "dth0")
-        halves = [(0, 2), (2, 4)]
-        neighbour(0, 0, v0[:], late[:, 0, :])
-        neighbour(0, 1, late[:, 1, :], late[:, 2, :])
-        add_turned(dth0, [freq_t[0], f[0][0]], 0, TILES, opens=True)
-        cross = bank("B4", "cross02")
-        gather_sn(0, 2, v2)
-        add_turned(cross, [v2], 0, TILES, opens=True)
-        add_turned(dth0, [f[0][1]], 0, TILES)
-        x2 = late[:, 4, :]
-        gather_cs(0, 2, x2, 0, TILES)
-        add_turned(cross, [x2], 0, TILES, closes=True)
-        normalise(1, *yz, rinv1)
-        weigh(2, f[0][2], cross, 0, TILES)
-        dth1 = [bank(tag, "dth1" + tag) for tag in ("B5", "B6")]
-        for h, half in enumerate(halves):
-            add_turned(dth1[h], [freq_t[1]], *half, opens=True)
-        add_turned(dth0, [f[0][2]], 0, TILES, closes=True)
-        q0 = damping(0, [dth0], [slice(0, S)])
+        weighted = [[held("weighted%d%d" % (b, d), [P, S], F32) for d in range(D)] for b in range(BLOCKS)]
+        first_term = held("first_term", [P, S], F32)
+        later_terms = held("later_terms", [P, 2 * D - 1, S], F32, on="r2_0")
+        terms = [first_term[:]] + [later_terms[:, n, :] for n in range(2 * D - 1)]
+        sn_terms, cs_terms = terms[0::2], terms[1::2]
+        dth0 = bank(7, "dth0")
+        neighbour(0, 0, sn_terms[0], cs_terms[0], HALVES)
+        neighbour(0, 1, sn_terms[1], cs_terms[1], [WHOLE])
+        add_turned(dth0, [freq_t[0], weighted[0][0]], WHOLE, opens=True)
+        cross = bank(4, "cross02")
+        gather_sn(0, 2, sn_terms[2], WHOLE)
+        add_turned(cross, [sn_terms[2]], WHOLE, opens=True)
+        add_turned(dth0, [weighted[0][1]], WHOLE)
+        gather_cs(0, 2, cs_terms[2], WHOLE)
+        add_turned(cross, [cs_terms[2]], WHOLE, closes=True)
 
-        v = [held("v1%d" % d, [P, S], F32) for d in range(D)]
-        x = [held("x1%d" % d, [P, S], F32) for d in range(D)]
-        last = [bank(tag, "cross12" + tag) for tag in ("B0", "B1")]
-        neighbour(1, 0, v[0][:], x[0][:])
-        cross = bank("B3", "cross11")
-        gather_sn(1, 1, v[1][:])
-        add_turned(cross, [v[1]], 0, TILES, opens=True)
-        for h, half in enumerate(halves):
-            add_turned(dth1[h], [f[1][0]], *half)
-        gather_cs(1, 1, x[1], 0, TILES)
-        add_turned(cross, [x[1]], 0, TILES, closes=True)
-        weigh(1, f[1][1], cross, 0, TILES)
-        gather_sn(1, 2, v[2][:])
-        for h, half in enumerate(halves):
-            add_turned(last[h], [v[2]], *half, opens=True)
-        for h, half in enumerate(halves):
-            gather_cs(1, 2, x[2], *half)
-            add_turned(last[h], [x[2]], *half, closes=True)
-            weigh(2, f[1][2], last[h], *half)
-            add_turned(dth1[h], [f[1][1]], *half)
-        for h, half in enumerate(halves):
-            add_turned(dth1[h], [f[1][2]], *half, closes=True)
-        finish(0, [dth0, dth0], q0)
-        finish(1, dth1, damping(1, dth1, HALF_COLS))
+        scale_by(sn[1], z, rinv, WHOLE)
+        for half in HALVES:
+            scale_by(cs[1], y, rinv, half)
+        negate_sn(1)
+        weigh(0, 2, cross, WHOLE)
+        dth1 = [bank(number, "dth1_%d" % number) for number in (5, 6)]
+        for h, half in enumerate(HALVES):
+            add_turned(dth1[h], [freq_t[1]], half, opens=True)
+        add_turned(dth0, [weighted[0][2]], WHOLE, closes=True)
+        damp0 = damping(0, [dth0], [WHOLE])
+
+        sn_terms = [held("sn_term1%d" % d, [P, S], F32) for d in range(D)]
+        cs_terms = [held("cs_term1%d" % d, [P, S], F32) for d in range(D)]
+        last_cross = [bank(number, "cross12_%d" % number) for number in (0, 1)]
+        neighbour(1, 0, sn_terms[0], cs_terms[0], HALVES)
+        cross = bank(3, "cross11")
+        gather_sn(1, 1, sn_terms[1], WHOLE)
+        add_turned(cross, [sn_terms[1]], WHOLE, opens=True)
+        for h, half in enumerate(HALVES):
+            add_turned(dth1[h], [weighted[1][0]], half)
+        gather_cs(1, 1, cs_terms[1], WHOLE)
+        add_turned(cross, [cs_terms[1]], WHOLE, closes=True)
+        weigh(1, 1, cross, WHOLE)
+        gather_sn(1, 2, sn_terms[2], WHOLE)
+        for h, half in enumerate(HALVES):
+            add_turned(last_cross[h], [sn_terms[2]], half, opens=True)
+        for h, half in enumerate(HALVES):
+            gather_cs(1, 2, cs_terms[2], half)
+            add_turned(last_cross[h], [cs_terms[2]], half, closes=True)
+            weigh(1, 2, last_cross[h], half)
+            add_turned(dth1[h], [weighted[1][1]], half)
+        for h, half in enumerate(HALVES):
+            add_turned(dth1[h], [weighted[1][2]], half, closes=True)
+
+        finish(0, [dth0, dth0], damp0)
+        finish(1, dth1, damping(1, dth1, HALVES))

from contextlib import ExitStack

import concourse.mybir as mybir
from concourse.masks import make_identity

K, T, S, N, D = 1024, 2048, 512, 256, 3
P = 128
PACK = 4
K_PASS = P * PACK
PASSES = K // K_PASS
BLOCKS = N // P
TILES = S // P
QUADRANT = 32
SCALE_ROWS = 4
GROUP = 16
LINE = 4
SPARE = 8
WHOLE = (0, TILES)
HALVES = ((0, TILES // 2), (TILES // 2, TILES))
FLOPS = 2 * 2 * K * N * S

F32 = mybir.dt.float32
BF16 = mybir.dt.bfloat16
I32 = mybir.dt.int32
U32 = mybir.dt.uint32
U16 = mybir.dt.uint16
U8 = mybir.dt.uint8
FP8X4 = mybir.dt.float8_e4m3fn_x4
ACT = mybir.ActivationFunctionType
MULT = mybir.AluOpType.mult
ADD = mybir.AluOpType.add


def cols(part):
    return slice(part[0] * P, part[1] * P)


def tile_picked_yphas_step_p_kernel(
    tc, x_words, x_scales, w1, w2, cpl, freq, offs, pos1, pos2, pos3, out
):
    nc = tc.nc
    with ExitStack() as ctx:
        keep = ctx.enter_context(tc.tile_pool(name="keep", bufs=1))
        psum = ctx.enter_context(tc.psum_pool(name="psum", bufs=1))

        def held(name, shape, dtype, on=None):
            return keep.tile(shape, dtype, name=name, tag=on or name, align_bytes=64)

        def bank(number, name):
            return psum.tile([P, S], F32, name=name, tag="bank%d" % number)

        x_tab = [held("x_tab%d" % o, [P, T], I32) for o in range(PASSES)]
        s_tab = held("s_tab", [P, T], U8)
        offs_sb = held("offs_sb", [P, S // GROUP], U16)
        pos_sb = [held("pos_sb%d" % d, [P, S // GROUP], U16) for d in range(D)]
        w_raw = {
            (b, i, o): held("w_raw%d%d%d" % (b, i, o), [P, PACK, P], F32)
            for b in range(BLOCKS) for i in range(2) for o in range(PASSES)
        }
        freq_sb = [held("freq_sb%d" % b, [P, S], F32) for b in range(BLOCKS)]
        cpl_rows = held("cpl_rows", [P, D, P], F32)
        ident = held("ident", [P, P], F32)

        nc.vector.memset(s_tab[:].bitcast(I32), 0)
        cs = [held("cs%d" % b, [P, S + SPARE], F32) for b in range(BLOCKS)]
        sn = [held("sn%d" % b, [P, S + SPARE], F32) for b in range(BLOCKS)]
        nc.vector.memset(cs[0][:, S:], 1.0)
        for window in (sn[0], cs[1], sn[1]):
            nc.scalar.activation(window[:, S:], cs[0][:, S:], ACT.Abs_reciprocal_sqrt)
        make_identity(nc, ident[:])
        nc.gpsimd.memset(cpl_rows[:], 0.0)

        def load_x(o):
            nc.sync.dma_start(x_tab[o][:], x_words[o].rearrange("p c r -> p (c r)").bitcast(I32))

        def load_w(b, o):
            for i, w in enumerate((w1, w2)):
                rows = w[o * K_PASS : (o + 1) * K_PASS, b * P : (b + 1) * P]
                nc.sync.dma_start(w_raw[b, i, o][:], rows.rearrange("(p j) n -> p j n", j=PACK))

        nc.sync.dma_start(offs_sb[:], offs)
        load_x(0)
        for q in range(P // QUADRANT):
            nc.sync.dma_start(
                s_tab[QUADRANT * q : QUADRANT * q + SCALE_ROWS * PASSES, :].bitcast(I32),
                x_scales[:, SCALE_ROWS * q : SCALE_ROWS * (q + 1), :].bitcast(I32),
            )
        load_w(0, 0)
        load_x(1)
        load_w(0, 1)
        load_w(1, 0)
        nc.sync.dma_start(cpl_rows[0:TILES, :, :], cpl[:, 0, :].rearrange("d (t p) -> t d p", p=P))
        load_w(1, 1)
        for d, pos in enumerate((pos1, pos2, pos3)):
            nc.sync.dma_start(pos_sb[d][:], pos)
        for b in range(BLOCKS):
            nc.sync.dma_start(freq_sb[b][:], freq[b * P : (b + 1) * P, :])

        x_codes = [held("x_codes%d" % o, [P, S], U32) for o in range(PASSES)]
        x_bytes = held("x_bytes", [P, S], U8)
        nc.vector.tensor_copy(x_codes[0][:], x_tab[0][:].bitcast(U32).indirect(offs_sb[:]))
        nc.vector.tensor_copy(x_bytes[:], s_tab[:].indirect(offs_sb[:]))
        nc.vector.tensor_copy(x_codes[1][:], x_tab[1][:].bitcast(U32).indirect(offs_sb[:]))

        w_codes, w_bytes = {}, {}

        def interleave(grouped, raw, copy):
            copy(grouped.rearrange("p (c n) j -> p c j n", n=LINE), raw.rearrange("p j (c n) -> p c j n", n=LINE))

        def quantise(grouped, keys, pieces=1):
            name = "%d%d%d" % keys[0]
            codes = held("w_codes" + name, [P, len(keys) * P], U32)
            scales = held("w_bytes" + name, [P, len(keys) * P], U8)
            width = len(keys) * P // pieces
            for h in range(pieces):
                c = slice(h * width, (h + 1) * width)
                nc.vector.quantize_mx(
                    out=codes[:, c].bitcast(FP8X4),
                    scales=scales[:, c],
                    in_=grouped[:, c, :].rearrange("p n j -> p (n j)"),
                )
            for n, key in enumerate(keys):
                w_codes[key] = codes[:, n * P : (n + 1) * P]
                w_bytes[key] = scales[:, n * P : (n + 1) * P]

        minus_sn = [held("minus_sn%d" % b, [P, S], F32) for b in range(BLOCKS)]

        def products(b, parts, y_banks, z_banks):
            yz = [
                [bank(number, "yz%d%d_%d" % (b, i, number)) for number in banks]
                for i, banks in enumerate((y_banks, z_banks))
            ]
            for o in range(PASSES):
                for i in range(2):
                    for acc, part in zip(yz[i], parts):
                        nc.tensor.matmul_mx(
                            out=acc[:, cols(part)],
                            lhsT=w_codes[b, i, o].bitcast(FP8X4),
                            lhsT_scale=w_bytes[b, i, o],
                            rhs=x_codes[o][:, cols(part)].bitcast(FP8X4),
                            rhs_scale=x_bytes[SCALE_ROWS * o :, cols(part)],
                            start=(o == 0),
                            stop=(o == PASSES - 1),
                        )
            return yz

        def add_turned(dst, srcs, part, opens=False, closes=False):
            steps = [(src, cols((t, t + 1))) for src in srcs for t in range(*part)]
            for n, (src, c) in enumerate(steps):
                nc.tensor.matmul(
                    dst[:, c], lhsT=src[:, c], rhs=ident[:], is_transpose=True,
                    start=(opens and n == 0), stop=(closes and n == len(steps) - 1),
                )

        def squares(b, yz, parts):
            sq = [held("sq%d%d" % (b, i), [P, S], F32) for i in range(2)]
            r2 = held("r2_%d" % b, [P, S], F32)
            rinv = held("rinv%d" % b, [P, S], F32)
            for i in range(2):
                for acc, part in zip(yz[i], parts):
                    nc.scalar.activation(sq[i][:, cols(part)], acc[:, cols(part)], ACT.Square)
            return sq, r2, rinv

        def inverse_radius(rinv, total, parts):
            for part in parts:
                nc.scalar.activation(rinv[:, cols(part)], total[:, cols(part)], ACT.Abs_reciprocal_sqrt, bias=0.1)

        def scale_by(window, acc, rinv, part):
            nc.vector.tensor_tensor(window[:, cols(part)], acc[:, cols(part)], rinv[:, cols(part)], MULT)

        def negate_sn(b):
            nc.scalar.activation(minus_sn[b][:], sn[b][:, :S], ACT.Copy, scale=-1.0)

        def places(d, part):
            return pos_sb[d][:, part[0] * P // GROUP : part[1] * P // GROUP]

        def gather_sn(b, d, term, part):
            nc.vector.tensor_tensor(term[:, cols(part)], sn[b][:].indirect(places(d, part)), cs[b][:, cols(part)], MULT)

        def gather_cs(b, d, term, part):
            nc.vector.tensor_tensor(
                term[:, cols(part)], cs[b][:].indirect(places(d, part)), minus_sn[b][:, cols(part)], MULT
            )

        def weigh(b, d, cross, part):
            for t in range(*part):
                c = cols((t, t + 1))
                nc.scalar.activation(weighted[b][d][:, c], cross[:, c], ACT.Copy, scale=cpl_t[:, d, t : t + 1])

        def neighbour(b, d, sn_term, cs_term, sn_parts):
            cross = bank(2 + d, "cross%d%d" % (b, d))
            for part in sn_parts:
                gather_sn(b, d, sn_term, part)
            add_turned(cross, [sn_term], WHOLE, opens=True)
            gather_cs(b, d, cs_term, WHOLE)
            add_turned(cross, [cs_term], WHOLE, closes=True)
            weigh(b, d, cross, WHOLE)

        def damping(b, dth, parts):
            a2, damp = [held("%s%d" % (name, b), [P, S], F32) for name in ("a2_", "damp")]
            for acc, part in zip(dth, parts):
                nc.scalar.activation(a2[:, cols(part)], acc[:, cols(part)], ACT.Square, scale=0.4)
            for part in parts:
                nc.scalar.activation(damp[:, cols(part)], a2[:, cols(part)], ACT.Abs_reciprocal_sqrt, bias=1.0)
            return damp

        def finish(b, dth, damp):
            pull, num = [held("%s%d" % (name, b), [P, S], F32) for name in ("pull", "num")]
            res = [held("res%d%d" % (b, h), [P, S // 2], F32) for h in range(2)]
            for acc, half in zip(dth, HALVES):
                c = cols(half)
                nc.vector.scalar_tensor_tensor(pull[:, c], acc[:, c], 0.4, minus_sn[b][:, c], MULT, MULT)
            for half in HALVES:
                c = cols(half)
                nc.vector.tensor_tensor(num[:, c], pull[:, c], cs[b][:, c], ADD)
            for h, half in enumerate(HALVES):
                c = cols(half)
                nc.vector.tensor_tensor(res[h][:], num[:, c], damp[:, c], MULT)
                nc.sync.dma_start(out[b * P : (b + 1) * P, c], res[h][:])

        for o in range(PASSES):
            for i in range(2):
                grouped = held("grouped0%d%d" % (i, o), [P, P, PACK], BF16)
                if (o, i) != (PASSES - 1, 1):
                    interleave(grouped[:], w_raw[0, i, o][:], nc.scalar.copy)
                    quantise(grouped[:], [(0, i, o)])
                else:
                    for c, copy in ((slice(0, P // 2), nc.vector.tensor_copy), (slice(P // 2, P), nc.scalar.copy)):
                        interleave(grouped[:, c, :], w_raw[0, i, o][:, :, c], copy)
                    quantise(grouped[:], [(0, i, o)], pieces=2)
        y, z = products(0, HALVES, (0, 2), (1, 7))
        sq, r2, rinv = squares(0, (y, z), HALVES)
        for half in HALVES:
            nc.vector.tensor_tensor(r2[:, cols(half)], sq[0][:, cols(half)], sq[1][:, cols(half)], ADD)
        inverse_radius(rinv, r2, HALVES)
        for h, half in enumerate(HALVES):
            scale_by(sn[0], z[h], rinv, half)
            scale_by(cs[0], y[h], rinv, half)
        negate_sn(0)

        cpl_t = held("cpl_t", [P, D, TILES], F32)
        cpl_bank = bank(5, "cpl_bank")
        for d in range(D):
            nc.tensor.transpose(cpl_bank[:, d * P : (d + 1) * P], cpl_rows[:, d, :], ident[:])
        nc.scalar.copy(cpl_t[:], cpl_bank[:].rearrange("p (d r) -> p d r", r=P)[:, 0:D, 0:TILES])
        freq_banks = []
        for b in range(BLOCKS):
            freq_banks.append(bank(5 + b, "freq_bank%d" % b))
            for t in range(TILES):
                c = cols((t, t + 1))
                nc.tensor.transpose(freq_banks[b][:, c], freq_sb[b][:, c], ident[:])

        grouped = [held("grouped1%d0" % i, [P, P, PACK], BF16) for i in range(2)]
        for i in range(2):
            interleave(grouped[i][:], w_raw[1, i, 0][:], nc.vector.tensor_copy)
        for i in range(2):
            quantise(grouped[i][:], [(1, i, 0)])
        grouped = held("grouped1_1", [P, 2 * P, PACK], BF16, on="r2_0")
        for i in range(2):
            interleave(grouped[:, i * P : (i + 1) * P, :], w_raw[1, i, 1][:], nc.scalar.copy)
        quantise(grouped[:], [(1, 0, 1), (1, 1, 1)])
        freq_t = []
        for b in range(BLOCKS):
            freq_t.append(held("freq_t%d" % b, [P, S], F32, on="w_raw1%d1" % (1 - b)))
            nc.scalar.copy(freq_t[b][:], freq_banks[b][:])
        (y,), (z,) = products(1, [WHOLE], (0,), (1,))
        sq, r2, rinv = squares(1, ([y], [z]), [WHOLE])
        r2_turned = bank(4, "r2_turned")
        add_turned(r2_turned, sq, WHOLE, opens=True, closes=True)
        nc.scalar.copy(r2[:], r2_turned[:])
        r2_back = bank(7, "r2_back")
        add_turned(r2_back, [r2], WHOLE, opens=True, closes=True)
        inverse_radius(rinv, r2_back, [WHOLE])

        weighted = [[held("weighted%d%d" % (b, d), [P, S], F32) for d in range(D)] for b in range(BLOCKS)]
        first_term = held("first_term", [P, S], F32)
        later_terms = held("later_terms", [P, 2 * D - 1, S], F32, on="r2_0")
        terms = [first_term[:]] + [later_terms[:, n, :] for n in range(2 * D - 1)]
        sn_terms, cs_terms = terms[0::2], terms[1::2]
        dth0 = bank(7, "dth0")
        neighbour(0, 0, sn_terms[0], cs_terms[0], HALVES)
        neighbour(0, 1, sn_terms[1], cs_terms[1], [WHOLE])
        add_turned(dth0, [freq_t[0], weighted[0][0]], WHOLE, opens=True)
        cross = bank(4, "cross02")
        gather_sn(0, 2, sn_terms[2], WHOLE)
        add_turned(cross, [sn_terms[2]], WHOLE, opens=True)
        add_turned(dth0, [weighted[0][1]], WHOLE)
        gather_cs(0, 2, cs_terms[2], WHOLE)
        add_turned(cross, [cs_terms[2]], WHOLE, closes=True)

        scale_by(sn[1], z, rinv, WHOLE)
        for half in HALVES:
            scale_by(cs[1], y, rinv, half)
        negate_sn(1)
        weigh(0, 2, cross, WHOLE)
        dth1 = [bank(number, "dth1_%d" % number) for number in (5, 6)]
        for h, half in enumerate(HALVES):
            add_turned(dth1[h], [freq_t[1]], half, opens=True)
        add_turned(dth0, [weighted[0][2]], WHOLE, closes=True)
        damp0 = damping(0, [dth0], [WHOLE])

        sn_terms = [held("sn_term1%d" % d, [P, S], F32) for d in range(D)]
        cs_terms = [held("cs_term1%d" % d, [P, S], F32) for d in range(D)]
        last_cross = [bank(number, "cross12_%d" % number) for number in (0, 1)]
        neighbour(1, 0, sn_terms[0], cs_terms[0], HALVES)
        cross = bank(3, "cross11")
        gather_sn(1, 1, sn_terms[1], WHOLE)
        add_turned(cross, [sn_terms[1]], WHOLE, opens=True)
        for h, half in enumerate(HALVES):
            add_turned(dth1[h], [weighted[1][0]], half)
        gather_cs(1, 1, cs_terms[1], WHOLE)
        add_turned(cross, [cs_terms[1]], WHOLE, closes=True)
        weigh(1, 1, cross, WHOLE)
        gather_sn(1, 2, sn_terms[2], WHOLE)
        for h, half in enumerate(HALVES):
            add_turned(last_cross[h], [sn_terms[2]], half, opens=True)
        for h, half in enumerate(HALVES):
            gather_cs(1, 2, cs_terms[2], half)
            add_turned(last_cross[h], [cs_terms[2]], half, closes=True)
            weigh(1, 2, last_cross[h], half)
            add_turned(dth1[h], [weighted[1][1]], half)
        for h, half in enumerate(HALVES):
            add_turned(dth1[h], [weighted[1][2]], half, closes=True)

        finish(0, [dth0, dth0], damp0)
        finish(1, dth1, damping(1, dth1, HALVES))
